import numpy as np
CORES = [65,66,69,71,193,194,197,199,321,322,325,327,449,450,453,455]
N = 16
GR, GC = 4, 4
L, KA, KB, F = 4, 1, 1, 128
def setup_inputs(rng):
    return {"a": rng.standard_normal((N, 128, KA * 128), dtype=np.float32), "b": rng.standard_normal((N, 128, KB * F), dtype=np.float32)}
def reference(a, b):
    A, B = a.astype(np.float64), b.astype(np.float64)
    y = np.zeros((N, 128, F))
    for i in range(GR):
        for j in range(GC):
            for k in range(L):
                At = A[i * GC + k // KA][:, 128 * (k % KA):128 * (k % KA) + 128]
                Bt = B[(k // KB) * GC + j][:, F * (k % KB):F * (k % KB) + F]
                y[i * GC + j] += At.T @ Bt
    return {"y": y.astype(np.float32 if a.dtype != np.float64 else np.float64)}

from concourse.bass import DstId, RemoteDMATransfer

GR, GC, W = 4, 4, 128

SCRATCH = {
    "abuf": ("sbuf", [128, GC * W], "float32"),
    "bbuf": ("sbuf", [128, GR * W], "float32"),
    "ysb": ("sbuf", [128, W], "float32"),
    "acc": ("psum", [128, W], "float32"),
}
SEMAPHORES = ["lda", "ldb", "arra", "bplane", "bcable", "bdiag", "sent", "mm", "cp", "st"]


def _count(mask):
    return sum((mask >> e) & 1 for e in range(mask.bit_length()))


def rank_program(g, core, T, topo):
    rank = T.rank_of(core)
    if rank is None:
        return
    S = T.sem
    i, j = rank // GC, rank % GC
    row = [T.cores[i * GC + k] for k in range(GC)]
    col = [T.cores[k * GC + j] for k in range(GR)]

    def a_slot(k):
        return T.abuf[:, k * W:(k + 1) * W]

    def b_slot(k):
        return T.bbuf[:, k * W:(k + 1) * W]

    def dst_id(d):
        rid, pid = topo.addr(d, core)
        return DstId(rid=rid, pnc=pid)

    others = [k for k in range(GR) if k != i]
    peers = [k for k in range(GC) if k != j]
    (plane,) = [k for k in others if topo.same_plane(core, col[k])]
    (cable,) = [k for k in others if topo.may_write(core, col[k]) and not topo.same_plane(core, col[k])]
    (diag,) = [k for k in others if not topo.may_write(core, col[k])]
    assert not topo.may_write(col[plane], col[cable])

    off = topo.mask(core, col[plane]) & topo.mask(core, col[cable])
    on = topo.mask(core, row[peers[0]])
    for k in peers:
        on &= topo.mask(core, row[k])
    a_mask = on & ~off
    n_off, n_a = _count(off), _count(a_mask)

    g.sync.dma_start(b_slot(i), T.b[:, :]).then_inc(S.ldb, 16)
    g.scalar.dma_start(a_slot(j), T.a[:, :]).then_inc(S.lda, 16)

    g.wait_ge(S.ldb, 16)
    rid, pid = topo.addr(col[plane], core)
    g.remote_dma(b_slot(i), b_slot(i), S.bplane, S.sent, pid, rid, off)
    g.wait_ge(S.lda, 16)
    g.remote_dma_fused([
        RemoteDMATransfer(dst_ids=[dst_id(col[cable])], dma_engine_mask=off, remote_sem=S.bcable,
                          src=b_slot(i), dst=b_slot(i)),
        RemoteDMATransfer(dst_ids=[dst_id(row[k]) for k in peers], dma_engine_mask=a_mask, remote_sem=S.arra,
                          srcs=[a_slot(j)], dsts=[a_slot(j) for k in peers]),
    ], local_sem=S.sent)
    g.wait_ge(S.bplane, n_off)
    rid, pid = topo.addr(col[cable], core)
    g.remote_dma(b_slot(plane), b_slot(plane), S.bdiag, S.sent, pid, rid, off)
    g.wait_ge(S.sent, 3 * n_off + n_a)

    te = g.tensor
    te.wait_ge(S.lda, 16)
    te.wait_ge(S.ldb, 16)
    te.wait_ge(S.arra, n_a * len(peers))
    te.matmul(T.acc[:, :], a_slot(i), b_slot(i), start=True, stop=False)
    te.wait_ge(S.bplane, n_off)
    te.matmul(T.acc[:, :], a_slot(plane), b_slot(plane), start=False, stop=False)
    te.wait_ge(S.bcable, n_off)
    te.matmul(T.acc[:, :], a_slot(cable), b_slot(cable), start=False, stop=False)
    te.wait_ge(S.bdiag, n_off)
    te.matmul(T.acc[:, :], a_slot(diag), b_slot(diag), start=False, stop=True).then_inc(S.mm, 1)

    g.vector.wait_ge(S.mm, 1)
    g.vector.tensor_copy(T.ysb[:, :], T.acc[:, :]).then_inc(S.cp, 1)
    g.sync.wait_ge(S.cp, 1)
    g.sync.dma_start(T.y[:, :], T.ysb[:, :]).then_inc(S.st, 16)
    g.sync.wait_ge(S.st, 16)
